import numpy as np
import ml_dtypes


def mxq(x, axis, fmt="e4m3"):
    dtype, down = {"e4m3": (ml_dtypes.float8_e4m3fn, 7), "e5m2": (ml_dtypes.float8_e5m2, 14)}[fmt]
    v = np.moveaxis(np.asarray(x, np.float32).astype(ml_dtypes.bfloat16).astype(np.float64), axis, -1)
    blocks = v.reshape(v.shape[:-1] + (-1, 32))
    amax = np.abs(blocks).max(-1, keepdims=True)
    byte = np.maximum(np.where(amax > 0, np.frexp(amax)[1] - 1 + 127, 0) - down, 1)
    scale = np.exp2(byte - 127.0)
    codes = (blocks / scale).astype(np.float32).astype(dtype).astype(np.float64)
    return np.moveaxis((codes * scale).reshape(v.shape), -1, axis)


WIDE = False


def mx_kscale(k):
    if not WIDE:
        return np.ones(k)
    levels = np.array([10, -10, 5, -5, 0])
    if k % 512:
        return np.exp2(np.random.permutation(np.resize(levels, k // 32))).repeat(32)
    a = np.empty((k // 512, 16))
    for p in range(k // 512):
        a[p, :8] = np.random.permutation(np.resize(levels, 8))
        for g in range(8):
            far = levels[np.abs(levels - a[p, g]) >= 10]
            a[p, g + 8] = far[np.random.randint(len(far))]
    return np.exp2(a.ravel()).repeat(32)


def f64(x):
    return np.asarray(x).astype(np.float64)


def striped(idx):
    return np.tile(idx.reshape(-1, 16).T, (8, 1)).astype(np.uint16)


def unstriped(offs):
    return offs[:16].T.reshape(-1).astype(np.int64)


E2M1 = np.array([0.0, 0.5, 1.0, 1.5, 2.0, 3.0, 4.0, 6.0, -0.0, -0.5, -1.0, -1.5, -2.0, -3.0, -4.0, -6.0])


def pack_weight(w, fmt):
    k, n = w.shape
    w = f64(np.asarray(w, np.float32).astype(ml_dtypes.bfloat16)).reshape(k // 32, 32, n)
    amax = np.abs(w).max(1)
    if fmt == "e4m3":
        byte = np.frexp(amax)[1] - 1 + 127 - 7
    else:
        mant, ex = np.frexp(amax / 6.0)
        byte = np.where(mant > 0.5, ex, ex - 1) + 127
    byte = np.clip(np.where(amax > 0, byte, 1), 1, 254)
    scaled = (w * np.exp2(127.0 - byte)[:, None, :]).reshape(k, n).astype(np.float32)
    by_word = np.ascontiguousarray(scaled.reshape(k // 512, 128, 4, n).transpose(0, 1, 3, 2))
    if fmt == "e4m3":
        words = by_word.astype(ml_dtypes.float8_e4m3fn).view(np.uint8)
    else:
        c = by_word.astype(ml_dtypes.float4_e2m1fn).view(np.uint8) & 0xF
        words = (c[..., 0::2] | (c[..., 1::2] << 4)).reshape(k // 512, 128, 2 * n)
    return np.ascontiguousarray(words), np.ascontiguousarray(byte.astype(np.uint8).reshape(k // 512, 16, n))


def unpack_weight(words, scales, fmt):
    g, _, n = scales.shape
    words = np.ascontiguousarray(words).reshape(g, 128, n, -1)
    if fmt == "e4m3":
        vals = words.view(ml_dtypes.float8_e4m3fn).astype(np.float64)
    else:
        nib = np.empty((g, 128, n, 4), np.uint8)
        nib[..., 0::2] = words & 0xF
        nib[..., 1::2] = words >> 4
        vals = E2M1[nib]
    vals = vals * np.repeat(np.exp2(scales.astype(np.float64) - 127.0), 8, axis=1)[..., None]
    return vals.transpose(0, 1, 3, 2).reshape(g * 512, n)


def gelu(v):
    return 0.5 * v * (1.0 + np.tanh(np.sqrt(2.0 / np.pi) * (v + 0.044715 * v**3)))


K, H, N, T, S, P = 512, 1536, 768, 4096, 1024, 512

def setup_inputs():
    n = np.random.standard_normal
    s = mx_kscale(K)[:, None]
    u = mx_kscale(H)[:, None]
    tab_words, tab_scales = pack_weight(n((K, T)) * s, "e4m3")
    w2_words, w2_scales = pack_weight(n((K, H)) / np.sqrt(K) / s * u.T, "e2m1")
    return {
        "tab_words": tab_words, "tab_scales": tab_scales,
        "offs": striped(np.random.permutation(T)[:S]),
        "pos1": striped(np.random.permutation(S)[:P]),
        "pos2": striped(np.random.permutation(S)[:P]),
        "w1": (0.85 * n((K, H)) / np.sqrt(K) / s).astype(np.float32),
        "w2_words": w2_words, "w2_scales": w2_scales,
        "cal": np.random.uniform(0.6, 3.0, H).astype(np.float32),
        "thr": n(H).astype(np.float32),
        "qual": (2.5 * n((H, P)) * u).astype(np.float32),
        "w3": (n((H, N)) / np.sqrt(H) / u).astype(np.float32),
    }

def reference(tab_words, tab_scales, offs, pos1, pos2, w1, w2_words, w2_scales, cal, thr, qual, w3):
    v = unpack_weight(tab_words, tab_scales, "e4m3")[:, unstriped(offs)]
    w2 = unpack_weight(w2_words, w2_scales, "e2m1")
    h = mxq(f64(w1), 0, "e4m3").T @ v
    g = w2.T @ v
    a = 1.0 / (1.0 + np.exp(-(f64(cal)[:, None] * h[:, unstriped(pos1)] + f64(thr)[:, None])))
    c = g[:, unstriped(pos2)]
    z = np.minimum(a * f64(qual), c)
    y = mxq(f64(w3), 0, "e4m3").T @ mxq(z, 0, "e4m3")
    return np.abs(y)

@@ -1,0 +1,274 @@
+from contextlib import ExitStack
+
+import concourse.mybir as mybir
+
+K, H, N, T, S, M = 512, 1536, 768, 4096, 1024, 512
+FLOPS = 2 * (2 * K * H * S + H * N * M)
+
+F32 = mybir.dt.float32
+BF16 = mybir.dt.bfloat16
+I32 = mybir.dt.int32
+U32 = mybir.dt.uint32
+U16 = mybir.dt.uint16
+U8 = mybir.dt.uint8
+FP8X4 = mybir.dt.float8_e4m3fn_x4
+FP4X4 = mybir.dt.float4_e2m1fn_x4
+ACT = mybir.ActivationFunctionType
+ALU = mybir.AluOpType
+
+P = 128
+PACK = 4
+PASS = P * PACK
+BLOCKS = H // PASS
+SLICES = BLOCKS * PACK
+BANK = 512
+HALF_M = M // 2
+HALF_N = N // 2
+G_LEAD = 4
+VECTOR_BANKS = 3
+
+
+def tile_list_elastography_evidence_kernel(
+    tc, tab_words, tab_scales, offs, pos1, pos2, w1, w2_words, w2_scales, cal, thr, qual, w3, out
+):
+    nc = tc.nc
+    with ExitStack() as ctx:
+        keep = ctx.enter_context(tc.tile_pool(name="keep", bufs=1))
+        work = ctx.enter_context(tc.tile_pool(name="work", bufs=2))
+        psum = ctx.enter_context(tc.psum_pool(name="psum", bufs=8))
+
+        offs_sb = keep.tile([P, S // 16], U16, name="offs_sb")
+        pos1_sb = keep.tile([P, M // 16], U16, name="pos1_sb")
+        pos2_sb = keep.tile([P, M // 16], U16, name="pos2_sb")
+        table_words = keep.tile([P, T], U32, name="table_words")
+        table_scales = keep.tile([P, T], U8, name="table_scales")
+        table_rows = keep.tile([P, T], U8, name="table_rows")
+        w2_raw_head = keep.tile([P, PASS], U16, name="w2_raw_head")
+        w2_raw_rest = keep.tile([P, H - PASS], U16, name="w2_raw_rest")
+        w2_raw_scales = keep.tile([P, H], U8, name="w2_raw_scales")
+        w2_codes = keep.tile([P, H], U16, name="w2_codes", align_bytes=64)
+        w2_plane = keep.tile([P, H], U8, name="w2_plane", align_bytes=64)
+        cal_sb = keep.tile([P, SLICES], F32, name="cal_sb")
+        thr_sb = keep.tile([P, SLICES], F32, name="thr_sb")
+        v_codes = [keep.tile([P, BANK], U32, name="v_codes%d" % u, align_bytes=64) for u in range(2)]
+        v_plane = [keep.tile([P, BANK], U8, name="v_plane%d" % u, align_bytes=64) for u in range(2)]
+        w1_raw = [keep.tile([P, PACK, PASS], F32, name="w1_raw%d" % b) for b in range(BLOCKS)]
+        w1_codes = [keep.tile([P, PASS], U32, name="w1_codes%d" % b, align_bytes=64) for b in range(BLOCKS)]
+        w1_plane = [keep.tile([P, PASS], U8, name="w1_plane%d" % b, align_bytes=64) for b in range(BLOCKS)]
+        w3_codes = [keep.tile([P, N], U32, name="w3_codes%d" % b, align_bytes=64) for b in range(BLOCKS)]
+        w3_plane = [keep.tile([P, N], U8, name="w3_plane%d" % b, align_bytes=64) for b in range(BLOCKS)]
+        z_codes = [keep.tile([P, M], U32, name="z_codes%d" % b, align_bytes=64) for b in range(BLOCKS)]
+        z_plane = [keep.tile([P, M], U8, name="z_plane%d" % b, align_bytes=64) for b in range(BLOCKS)]
+        score = [keep.tile([P, PACK, M], F32, name="score%d" % b) for b in range(BLOCKS)]
+        w3_raw, cap, h_rows, g_rows, gate = {}, {}, {}, {}, {}
+
+        nc.vector.memset(table_scales[:].bitcast(I32), 0)
+        nc.gpsimd.memset(w2_raw_scales[:].bitcast(I32), 0)
+        for q in range(4):
+            nc.sync.dma_start(table_rows[32 * q : 32 * q + 4, :].bitcast(I32), tab_scales[0, 4 * q : 4 * q + 4, :].bitcast(I32))
+        nc.sync.dma_start(offs_sb[:], offs)
+        nc.sync.dma_start(w2_raw_head[:].bitcast(I32), w2_words[0, :, : 2 * PASS].bitcast(I32))
+        nc.sync.dma_start(table_words[:].bitcast(I32), tab_words[0].rearrange("p n t -> p (n t)").bitcast(I32))
+        for q in range(4):
+            nc.gpsimd.dma_start(w2_raw_scales[32 * q : 32 * q + 4, :].bitcast(I32), w2_scales[0, 4 * q : 4 * q + 4, :].bitcast(I32))
+
+        def load_w1(b):
+            nc.sync.dma_start(w1_raw[b][:], w1[:, b * PASS : (b + 1) * PASS].rearrange("(p j) c -> p j c", j=PACK))
+
+        def load_qual(b):
+            nc.sync.dma_start(score[b][:], qual[b * PASS : (b + 1) * PASS, :].rearrange("(p t) m -> p t m", t=PACK))
+
+        def load_w3(b):
+            w3_raw[b] = work.tile([P, PACK, N], F32, name="w3_raw")
+            nc.sync.dma_start(w3_raw[b][:], w3[b * PASS : (b + 1) * PASS, :].rearrange("(p t) n -> p t n", t=PACK))
+
+        load_w1(0)
+        nc.sync.dma_start(pos2_sb[:], pos2)
+        nc.sync.dma_start(pos1_sb[:], pos1)
+        nc.sync.dma_start(cal_sb[:].rearrange("p (b t) -> p b t", t=PACK), cal.rearrange("(b p t) -> p b t", p=P, t=PACK))
+        nc.sync.dma_start(thr_sb[:].rearrange("p (b t) -> p b t", t=PACK), thr.rearrange("(b p t) -> p b t", p=P, t=PACK))
+        nc.sync.dma_start(w2_raw_rest[:].bitcast(I32), w2_words[0, :, 2 * PASS :].bitcast(I32))
+        load_qual(0)
+        load_w1(1)
+        load_w3(0)
+        load_qual(1)
+        load_w1(2)
+        load_w3(1)
+        load_qual(2)
+
+        def deal_words(raw, cols):
+            nc.scalar.copy(
+                out=w2_codes[:, cols].rearrange("p (b t m) -> p b t m", t=PACK, m=P),
+                in_=raw[:].rearrange("p (b m t) -> p b t m", t=PACK, m=P),
+            )
+
+        def deal_scales(cols):
+            nc.vector.tensor_copy(
+                out=w2_plane[:, cols].rearrange("p (b t m) -> p b t m", t=PACK, m=P),
+                in_=w2_raw_scales[:, cols].rearrange("p (b m t) -> p b t m", t=PACK, m=P),
+            )
+
+        for q in range(4):
+            rows = slice(32 * q, 32 * q + 4)
+            nc.vector.tensor_copy(out=table_scales[rows, :].bitcast(I32), in_=table_rows[rows, :].bitcast(I32))
+        deal_words(w2_raw_head, slice(0, PASS))
+        for u in range(2):
+            nc.vector.tensor_copy(out=v_plane[u][:], in_=table_scales[:].indirect(offs_sb[:, 32 * u : 32 * u + 32]))
+        deal_scales(slice(0, PASS))
+        for u in range(2):
+            nc.vector.tensor_copy(out=v_codes[u][:], in_=table_words[:].indirect(offs_sb[:, 32 * u : 32 * u + 32]))
+
+        def round_w1(b):
+            rounded = work.tile([P, PACK * PASS], BF16, name="rounded", align_bytes=64)
+            nc.vector.tensor_copy(
+                out=rounded[:].rearrange("p (t m j) -> p m j t", t=PACK, j=PACK),
+                in_=w1_raw[b][:].rearrange("p j (m t) -> p m j t", t=PACK),
+            )
+            return rounded
+
+        def quantize_w1(b, rounded):
+            nc.vector.quantize_mx(out=w1_codes[b][:].bitcast(FP8X4), scales=w1_plane[b][:], in_=rounded[:])
+
+        def round_w3(b, u):
+            rounded = work.tile([P, PACK * HALF_N], BF16, name="rounded", align_bytes=64)
+            nc.vector.tensor_copy(
+                out=rounded[:].rearrange("p (c i t) -> p c t i", i=4, t=PACK),
+                in_=w3_raw[b][:, :, u * HALF_N : (u + 1) * HALF_N].rearrange("p t (c i) -> p c t i", i=4),
+            )
+            return rounded
+
+        def quantize_w3(b, u, rounded):
+            cols = slice(u * HALF_N, (u + 1) * HALF_N)
+            nc.vector.quantize_mx(out=w3_codes[b][:, cols].bitcast(FP8X4), scales=w3_plane[b][:, cols], in_=rounded[:])
+
+        def g_half(s, u):
+            if u == 0:
+                g_rows[s] = work.tile([P, S], F32, name="g_rows", bufs=5)
+            cols = slice(s * P, (s + 1) * P)
+            acc = psum.tile([P, BANK], F32, name="bank")
+            nc.tensor.matmul_mx(
+                out=acc[:], lhsT=w2_codes[:, cols].bitcast(FP4X4), lhsT_scale=w2_plane[:, cols],
+                rhs=v_codes[u][:].bitcast(FP8X4), rhs_scale=v_plane[u][:], start=True, stop=True,
+            )
+            if u == 1 and s >= SLICES - VECTOR_BANKS:
+                nc.vector.tensor_copy(out=g_rows[s][:, u * BANK : (u + 1) * BANK], in_=acc[:])
+            else:
+                nc.scalar.copy(out=g_rows[s][:, u * BANK : (u + 1) * BANK], in_=acc[:])
+
+        def h_half(s, u):
+            b, t = divmod(s, PACK)
+            if u == 0:
+                h_rows[s] = work.tile([P, S], F32, name="h_rows", bufs=3)
+            cols = slice(t * P, (t + 1) * P)
+            acc = psum.tile([P, BANK], F32, name="bank")
+            nc.tensor.matmul_mx(
+                out=acc[:], lhsT=w1_codes[b][:, cols].bitcast(FP8X4), lhsT_scale=w1_plane[b][:, cols],
+                rhs=v_codes[u][:].bitcast(FP8X4), rhs_scale=v_plane[u][:], start=True, stop=True,
+            )
+            nc.scalar.copy(out=h_rows[s][:, u * BANK : (u + 1) * BANK], in_=acc[:])
+
+        def look(s, lo, hi):
+            if lo == 0:
+                gate[s] = work.tile([P, M], F32, name="gate", bufs=3)
+            nc.scalar.activation(
+                out=gate[s][:, lo:hi], in_=h_rows[s][:].indirect(pos1_sb[:, lo // 16 : hi // 16]), func=ACT.Sigmoid,
+                bias=thr_sb[:, s : s + 1], scale=cal_sb[:, s : s + 1],
+            )
+
+        def pick(s):
+            b, t = divmod(s, PACK)
+            if t == 0:
+                cap[b] = work.tile([P, PACK, M], F32, name="cap")
+            nc.vector.tensor_copy(out=cap[b][:, t, :], in_=g_rows[s][:].indirect(pos2_sb[:]))
+
+        def weigh(s, lo, hi):
+            b, t = divmod(s, PACK)
+            nc.vector.tensor_tensor(out=score[b][:, t, lo:hi], in0=gate[s][:, lo:hi], in1=score[b][:, t, lo:hi], op=ALU.mult)
+
+        def cap_score(b, u):
+            cols = slice(u * HALF_M, (u + 1) * HALF_M)
+            z = work.tile([P, PACK * HALF_M], BF16, name="z", align_bytes=64)
+            nc.vector.tensor_tensor(
+                out=z[:].rearrange("p (c i t) -> p c t i", i=4, t=PACK),
+                in0=score[b][:, :, cols].rearrange("p t (c i) -> p c t i", i=4),
+                in1=cap[b][:, :, cols].rearrange("p t (c i) -> p c t i", i=4),
+                op=ALU.min,
+            )
+            return z
+
+        def quantize_z(b, u, z):
+            cols = slice(u * HALF_M, (u + 1) * HALF_M)
+            nc.vector.quantize_mx(out=z_codes[b][:, cols].bitcast(FP8X4), scales=z_plane[b][:, cols], in_=z[:])
+
+        for u in range(2):
+            for s in range(G_LEAD):
+                g_half(s, u)
+        quantize_w1(0, round_w1(0))
+        deal_words(w2_raw_rest, slice(PASS, H))
+        deal_scales(slice(PASS, H))
+        h_half(0, 0)
+        h_half(0, 1)
+
+        weight_jobs = {0: (1, None), 1: (0, 0), 2: (0, 1), 3: (2, None), 4: (1, 0), 5: (1, 1), 7: (2, 0), 8: (2, 1)}
+        last = SLICES - 1
+        for s in range(SLICES):
+            b, t = divmod(s, PACK)
+            pick(s)
+            if s < last:
+                h_half(s + 1, 0)
+                h_half(s + 1, 1)
+                look(s, 0, M)
+            else:
+                look(s, 0, HALF_M)
+                look(s, HALF_M, M)
+            if s + G_LEAD < SLICES:
+                g_half(s + G_LEAD, 0)
+                g_half(s + G_LEAD, 1)
+            job = weight_jobs.get(s)
+            if job is not None:
+                rounded = round_w1(job[0]) if job[1] is None else round_w3(*job)
+            if s < last:
+                weigh(s, 0, M)
+            if job is not None:
+                if job[1] is None:
+                    quantize_w1(job[0], rounded)
+                else:
+                    quantize_w3(job[0], job[1], rounded)
+            if s == 2:
+                load_w3(2)
+            if t == PACK - 1 and s < last:
+                z0 = cap_score(b, 0)
+                z1 = cap_score(b, 1)
+                quantize_z(b, 0, z0)
+                quantize_z(b, 1, z1)
+
+        accs = {}
+
+        def second(u, pair, b):
+            if b == 0:
+                accs[u, pair] = psum.tile([P, BANK], F32, name="bank")
+            for e in range(2):
+                n_cols = slice((2 * pair + e) * P, (2 * pair + e + 1) * P)
+                m_cols = slice(u * HALF_M, (u + 1) * HALF_M)
+                nc.tensor.matmul_mx(
+                    out=accs[u, pair][:, e * HALF_M : (e + 1) * HALF_M],
+                    lhsT=w3_codes[b][:, n_cols].bitcast(FP8X4), lhsT_scale=w3_plane[b][:, n_cols],
+                    rhs=z_codes[b][:, m_cols].bitcast(FP8X4), rhs_scale=z_plane[b][:, m_cols],
+                    start=(b == 0 and e == 0), stop=(b == BLOCKS - 1 and e == 1),
+                )
+
+        for u in range(2):
+            for pair in range(3):
+                for b in range(BLOCKS - 1):
+                    second(u, pair, b)
+        for u in range(2):
+            weigh(last, u * HALF_M, (u + 1) * HALF_M)
+            quantize_z(BLOCKS - 1, u, cap_score(BLOCKS - 1, u))
+            for pair in range(3):
+                second(u, pair, BLOCKS - 1)
+                result = work.tile([P, 2, HALF_M], F32, name="result", bufs=6)
+                nc.scalar.activation(out=result[:].rearrange("p e m -> p (e m)"), in_=accs[u, pair][:], func=ACT.Abs)
+                nc.sync.dma_start(
+                    out[2 * pair * P : (2 * pair + 2) * P, u * HALF_M : (u + 1) * HALF_M].rearrange("(e p) m -> p e m", p=P),
+                    result[:],
+                )

@@ -25,7 +25,7 @@ BANK = 512
 HALF_M = M // 2
 HALF_N = N // 2
 G_LEAD = 4
-VECTOR_BANKS = 3
+VECTOR_BANKS = 0
 
 
 def tile_list_elastography_evidence_kernel(
@@ -43,8 +43,8 @@ def tile_list_elastography_evidence_kernel(
         table_words = keep.tile([P, T], U32, name="table_words")
         table_scales = keep.tile([P, T], U8, name="table_scales")
         table_rows = keep.tile([P, T], U8, name="table_rows")
-        w2_raw_head = keep.tile([P, PASS], U16, name="w2_raw_head")
-        w2_raw_rest = keep.tile([P, H - PASS], U16, name="w2_raw_rest")
+        w2_rows = keep.tile([P, H], U8, name="w2_rows")
+        w2_raw_words = keep.tile([P, H], U16, name="w2_raw_words")
         w2_raw_scales = keep.tile([P, H], U8, name="w2_raw_scales")
         w2_codes = keep.tile([P, H], U16, name="w2_codes", align_bytes=64)
         w2_plane = keep.tile([P, H], U8, name="w2_plane", align_bytes=64)
@@ -67,10 +67,10 @@ def tile_list_elastography_evidence_kernel(
         for q in range(4):
             nc.sync.dma_start(table_rows[32 * q : 32 * q + 4, :].bitcast(I32), tab_scales[0, 4 * q : 4 * q + 4, :].bitcast(I32))
         nc.sync.dma_start(offs_sb[:], offs)
-        nc.sync.dma_start(w2_raw_head[:].bitcast(I32), w2_words[0, :, : 2 * PASS].bitcast(I32))
+        nc.sync.dma_start(w2_raw_words[:].bitcast(I32), w2_words[0].bitcast(I32))
         nc.sync.dma_start(table_words[:].bitcast(I32), tab_words[0].rearrange("p n t -> p (n t)").bitcast(I32))
         for q in range(4):
-            nc.gpsimd.dma_start(w2_raw_scales[32 * q : 32 * q + 4, :].bitcast(I32), w2_scales[0, 4 * q : 4 * q + 4, :].bitcast(I32))
+            nc.sync.dma_start(w2_rows[32 * q : 32 * q + 4, :].bitcast(I32), w2_scales[0, 4 * q : 4 * q + 4, :].bitcast(I32))
 
         def load_w1(b):
             nc.sync.dma_start(w1_raw[b][:], w1[:, b * PASS : (b + 1) * PASS].rearrange("(p j) c -> p j c", j=PACK))
@@ -87,7 +87,6 @@ def tile_list_elastography_evidence_kernel(
         nc.sync.dma_start(pos1_sb[:], pos1)
         nc.sync.dma_start(cal_sb[:].rearrange("p (b t) -> p b t", t=PACK), cal.rearrange("(b p t) -> p b t", p=P, t=PACK))
         nc.sync.dma_start(thr_sb[:].rearrange("p (b t) -> p b t", t=PACK), thr.rearrange("(b p t) -> p b t", p=P, t=PACK))
-        nc.sync.dma_start(w2_raw_rest[:].bitcast(I32), w2_words[0, :, 2 * PASS :].bitcast(I32))
         load_qual(0)
         load_w1(1)
         load_w3(0)
@@ -111,12 +110,15 @@ def tile_list_elastography_evidence_kernel(
         for q in range(4):
             rows = slice(32 * q, 32 * q + 4)
             nc.vector.tensor_copy(out=table_scales[rows, :].bitcast(I32), in_=table_rows[rows, :].bitcast(I32))
-        deal_words(w2_raw_head, slice(0, PASS))
+        deal_words(w2_raw_words, slice(0, H))
         for u in range(2):
             nc.vector.tensor_copy(out=v_plane[u][:], in_=table_scales[:].indirect(offs_sb[:, 32 * u : 32 * u + 32]))
+        for q in range(4):
+            rows = slice(32 * q, 32 * q + 4)
+            nc.scalar.copy(out=w2_raw_scales[rows, :].bitcast(U32), in_=w2_rows[rows, :].bitcast(U32))
+        nc.vector.tensor_copy(out=v_codes[0][:], in_=table_words[:].indirect(offs_sb[:, 0:32]))
         deal_scales(slice(0, PASS))
-        for u in range(2):
-            nc.vector.tensor_copy(out=v_codes[u][:], in_=table_words[:].indirect(offs_sb[:, 32 * u : 32 * u + 32]))
+        nc.vector.tensor_copy(out=v_codes[1][:], in_=table_words[:].indirect(offs_sb[:, 32:64]))
 
         def round_w1(b):
             rounded = work.tile([P, PACK * PASS], BF16, name="rounded", align_bytes=64)
@@ -185,9 +187,9 @@ def tile_list_elastography_evidence_kernel(
             b, t = divmod(s, PACK)
             nc.vector.tensor_tensor(out=score[b][:, t, lo:hi], in0=gate[s][:, lo:hi], in1=score[b][:, t, lo:hi], op=ALU.mult)
 
-        def cap_score(b, u):
-            cols = slice(u * HALF_M, (u + 1) * HALF_M)
-            z = work.tile([P, PACK * HALF_M], BF16, name="z", align_bytes=64)
+        def cap_score(b, lo, hi):
+            cols = slice(lo, hi)
+            z = work.tile([P, PACK * (hi - lo)], BF16, name="z", align_bytes=64, bufs=3)
             nc.vector.tensor_tensor(
                 out=z[:].rearrange("p (c i t) -> p c t i", i=4, t=PACK),
                 in0=score[b][:, :, cols].rearrange("p t (c i) -> p c t i", i=4),
@@ -196,15 +198,14 @@ def tile_list_elastography_evidence_kernel(
             )
             return z
 
-        def quantize_z(b, u, z):
-            cols = slice(u * HALF_M, (u + 1) * HALF_M)
+        def quantize_z(b, lo, hi, z):
+            cols = slice(lo, hi)
             nc.vector.quantize_mx(out=z_codes[b][:, cols].bitcast(FP8X4), scales=z_plane[b][:, cols], in_=z[:])
 
         for u in range(2):
             for s in range(G_LEAD):
                 g_half(s, u)
         quantize_w1(0, round_w1(0))
-        deal_words(w2_raw_rest, slice(PASS, H))
         deal_scales(slice(PASS, H))
         h_half(0, 0)
         h_half(0, 1)
@@ -237,38 +238,48 @@ def tile_list_elastography_evidence_kernel(
             if s == 2:
                 load_w3(2)
             if t == PACK - 1 and s < last:
-                z0 = cap_score(b, 0)
-                z1 = cap_score(b, 1)
-                quantize_z(b, 0, z0)
-                quantize_z(b, 1, z1)
+                z0 = cap_score(b, 0, HALF_M)
+                z1 = cap_score(b, HALF_M, M)
+                quantize_z(b, 0, HALF_M, z0)
+                quantize_z(b, HALF_M, M, z1)
 
+        pieces = ((0, HALF_M, 2), (HALF_M, HALF_M + P, 3), (HALF_M + P, M, 3))
         accs = {}
 
-        def second(u, pair, b):
+        def second(lo, hi, tiles, first, b):
+            width = hi - lo
             if b == 0:
-                accs[u, pair] = psum.tile([P, BANK], F32, name="bank")
-            for e in range(2):
-                n_cols = slice((2 * pair + e) * P, (2 * pair + e + 1) * P)
-                m_cols = slice(u * HALF_M, (u + 1) * HALF_M)
+                accs[lo, first] = psum.tile([P, BANK], F32, name="bank")
+            for e in range(tiles):
+                n_cols = slice((first + e) * P, (first + e + 1) * P)
                 nc.tensor.matmul_mx(
-                    out=accs[u, pair][:, e * HALF_M : (e + 1) * HALF_M],
+                    out=accs[lo, first][:, e * width : (e + 1) * width],
                     lhsT=w3_codes[b][:, n_cols].bitcast(FP8X4), lhsT_scale=w3_plane[b][:, n_cols],
-                    rhs=z_codes[b][:, m_cols].bitcast(FP8X4), rhs_scale=z_plane[b][:, m_cols],
-                    start=(b == 0 and e == 0), stop=(b == BLOCKS - 1 and e == 1),
+                    rhs=z_codes[b][:, lo:hi].bitcast(FP8X4), rhs_scale=z_plane[b][:, lo:hi],
+                    start=(b == 0 and e == 0), stop=(b == BLOCKS - 1 and e == tiles - 1),
                 )
 
-        for u in range(2):
-            for pair in range(3):
-                for b in range(BLOCKS - 1):
-                    second(u, pair, b)
-        for u in range(2):
-            weigh(last, u * HALF_M, (u + 1) * HALF_M)
-            quantize_z(BLOCKS - 1, u, cap_score(BLOCKS - 1, u))
-            for pair in range(3):
-                second(u, pair, BLOCKS - 1)
-                result = work.tile([P, 2, HALF_M], F32, name="result", bufs=6)
-                nc.scalar.activation(out=result[:].rearrange("p e m -> p (e m)"), in_=accs[u, pair][:], func=ACT.Abs)
-                nc.sync.dma_start(
-                    out[2 * pair * P : (2 * pair + 2) * P, u * HALF_M : (u + 1) * HALF_M].rearrange("(e p) m -> p e m", p=P),
-                    result[:],
+        def finish(lo, hi, tiles):
+            width = hi - lo
+            for first in range(0, N // P, tiles):
+                second(lo, hi, tiles, first, BLOCKS - 1)
+                result = work.tile([P, tiles, width], F32, name="result", bufs=7)
+                nc.scalar.activation(
+                    out=result[:].rearrange("p e m -> p (e m)"), in_=accs[lo, first][:, : tiles * width], func=ACT.Abs
                 )
+                nc.sync.dma_start(
+                    out[first * P : (first + tiles) * P, lo:hi].rearrange("(e p) m -> p e m", p=P), result[:]
+                )
+
+        for lo, hi, tiles in pieces:
+            for first in range(0, N // P, tiles):
+                for b in range(BLOCKS - 1):
+                    second(lo, hi, tiles, first, b)
+        weigh(last, 0, HALF_M)
+        z_parts = [cap_score(BLOCKS - 1, 0, HALF_M)]
+        weigh(last, HALF_M, M)
+        for index, (lo, hi, tiles) in enumerate(pieces):
+            quantize_z(BLOCKS - 1, lo, hi, z_parts[index])
+            if index == 0:
+                z_parts.extend(cap_score(BLOCKS - 1, lo2, hi2) for lo2, hi2, tiles2 in pieces[1:])
+            finish(lo, hi, tiles)

@@ -26,6 +26,8 @@ HALF_M = M // 2
 HALF_N = N // 2
 G_LEAD = 4
 VECTOR_BANKS = 0
+PICK_LEAD = 3
+SCALAR_ROUNDS = ((2, 0),)
 
 
 def tile_list_elastography_evidence_kernel(
@@ -133,9 +135,10 @@ def tile_list_elastography_evidence_kernel(
 
         def round_w3(b, u):
             rounded = work.tile([P, PACK * HALF_N], BF16, name="rounded", align_bytes=64)
-            nc.vector.tensor_copy(
-                out=rounded[:].rearrange("p (c i t) -> p c t i", i=4, t=PACK),
-                in_=w3_raw[b][:, :, u * HALF_N : (u + 1) * HALF_N].rearrange("p t (c i) -> p c t i", i=4),
+            copy = nc.scalar.copy if (b, u) in SCALAR_ROUNDS else nc.vector.tensor_copy
+            copy(
+                out=rounded[:].rearrange("p (c i t) -> p c t i", i=2, t=PACK),
+                in_=w3_raw[b][:, :, u * HALF_N : (u + 1) * HALF_N].rearrange("p t (c i) -> p c t i", i=2),
             )
             return rounded
 
@@ -145,35 +148,34 @@ def tile_list_elastography_evidence_kernel(
 
         def g_half(s, u):
             if u == 0:
-                g_rows[s] = work.tile([P, S], F32, name="g_rows", bufs=5)
+                g_rows[s] = work.tile([P, S], F32, name="g_rows", bufs=4)
             cols = slice(s * P, (s + 1) * P)
             acc = psum.tile([P, BANK], F32, name="bank")
             nc.tensor.matmul_mx(
                 out=acc[:], lhsT=w2_codes[:, cols].bitcast(FP4X4), lhsT_scale=w2_plane[:, cols],
                 rhs=v_codes[u][:].bitcast(FP8X4), rhs_scale=v_plane[u][:], start=True, stop=True,
             )
-            if u == 1 and s >= SLICES - VECTOR_BANKS:
-                nc.vector.tensor_copy(out=g_rows[s][:, u * BANK : (u + 1) * BANK], in_=acc[:])
-            else:
-                nc.scalar.copy(out=g_rows[s][:, u * BANK : (u + 1) * BANK], in_=acc[:])
+            nc.scalar.copy(out=g_rows[s][:, u * BANK : (u + 1) * BANK], in_=acc[:])
 
         def h_half(s, u):
             b, t = divmod(s, PACK)
             if u == 0:
-                h_rows[s] = work.tile([P, S], F32, name="h_rows", bufs=3)
+                h_rows[s] = work.tile([P, S], F32, name="h_rows", bufs=5)
             cols = slice(t * P, (t + 1) * P)
             acc = psum.tile([P, BANK], F32, name="bank")
             nc.tensor.matmul_mx(
                 out=acc[:], lhsT=w1_codes[b][:, cols].bitcast(FP8X4), lhsT_scale=w1_plane[b][:, cols],
                 rhs=v_codes[u][:].bitcast(FP8X4), rhs_scale=v_plane[u][:], start=True, stop=True,
             )
-            nc.scalar.copy(out=h_rows[s][:, u * BANK : (u + 1) * BANK], in_=acc[:])
+            if u == 1 and s >= SLICES - VECTOR_BANKS:
+                nc.vector.tensor_copy(out=h_rows[s][:, u * BANK : (u + 1) * BANK], in_=acc[:])
+            else:
+                nc.scalar.copy(out=h_rows[s][:, u * BANK : (u + 1) * BANK], in_=acc[:])
 
         def look(s, lo, hi):
-            if lo == 0:
-                gate[s] = work.tile([P, M], F32, name="gate", bufs=3)
+            gate[s, lo] = work.tile([P, hi - lo], F32, name="gate", bufs=4)
             nc.scalar.activation(
-                out=gate[s][:, lo:hi], in_=h_rows[s][:].indirect(pos1_sb[:, lo // 16 : hi // 16]), func=ACT.Sigmoid,
+                out=gate[s, lo][:], in_=h_rows[s][:].indirect(pos1_sb[:, lo // 16 : hi // 16]), func=ACT.Sigmoid,
                 bias=thr_sb[:, s : s + 1], scale=cal_sb[:, s : s + 1],
             )
 
@@ -185,15 +187,15 @@ def tile_list_elastography_evidence_kernel(
 
         def weigh(s, lo, hi):
             b, t = divmod(s, PACK)
-            nc.vector.tensor_tensor(out=score[b][:, t, lo:hi], in0=gate[s][:, lo:hi], in1=score[b][:, t, lo:hi], op=ALU.mult)
+            nc.vector.tensor_tensor(out=score[b][:, t, lo:hi], in0=gate[s, lo][:], in1=score[b][:, t, lo:hi], op=ALU.mult)
 
         def cap_score(b, lo, hi):
             cols = slice(lo, hi)
             z = work.tile([P, PACK * (hi - lo)], BF16, name="z", align_bytes=64, bufs=3)
             nc.vector.tensor_tensor(
-                out=z[:].rearrange("p (c i t) -> p c t i", i=4, t=PACK),
-                in0=score[b][:, :, cols].rearrange("p t (c i) -> p c t i", i=4),
-                in1=cap[b][:, :, cols].rearrange("p t (c i) -> p c t i", i=4),
+                out=z[:].rearrange("p (c i t) -> p c t i", i=2, t=PACK),
+                in0=score[b][:, :, cols].rearrange("p t (c i) -> p c t i", i=2),
+                in1=cap[b][:, :, cols].rearrange("p t (c i) -> p c t i", i=2),
                 op=ALU.min,
             )
             return z
@@ -210,34 +212,35 @@ def tile_list_elastography_evidence_kernel(
         h_half(0, 0)
         h_half(0, 1)
 
-        weight_jobs = {0: (1, None), 1: (0, 0), 2: (0, 1), 3: (2, None), 4: (1, 0), 5: (1, 1), 7: (2, 0), 8: (2, 1)}
-        last = SLICES - 1
+        for s in range(PICK_LEAD):
+            pick(s)
+
+        weight_jobs = {1: (1, None), 2: (0, 0), 3: (0, 1), 4: (2, None), 5: (1, 0), 6: (1, 1), 8: (2, 0), 9: (2, 1)}
+        split = SLICES - PACK
         for s in range(SLICES):
             b, t = divmod(s, PACK)
-            pick(s)
-            if s < last:
+            width = M if s < split else HALF_M
+            if s + 1 < SLICES:
                 h_half(s + 1, 0)
                 h_half(s + 1, 1)
-                look(s, 0, M)
-            else:
-                look(s, 0, HALF_M)
-                look(s, HALF_M, M)
+            look(s, 0, width)
             if s + G_LEAD < SLICES:
                 g_half(s + G_LEAD, 0)
                 g_half(s + G_LEAD, 1)
             job = weight_jobs.get(s)
             if job is not None:
                 rounded = round_w1(job[0]) if job[1] is None else round_w3(*job)
-            if s < last:
-                weigh(s, 0, M)
+            if s + PICK_LEAD < SLICES:
+                pick(s + PICK_LEAD)
             if job is not None:
                 if job[1] is None:
                     quantize_w1(job[0], rounded)
                 else:
                     quantize_w3(job[0], job[1], rounded)
-            if s == 2:
+            weigh(s, 0, width)
+            if job == (0, 1):
                 load_w3(2)
-            if t == PACK - 1 and s < last:
+            if t == PACK - 1 and s < split:
                 z0 = cap_score(b, 0, HALF_M)
                 z1 = cap_score(b, HALF_M, M)
                 quantize_z(b, 0, HALF_M, z0)
@@ -275,11 +278,14 @@ def tile_list_elastography_evidence_kernel(
             for first in range(0, N // P, tiles):
                 for b in range(BLOCKS - 1):
                     second(lo, hi, tiles, first, b)
-        weigh(last, 0, HALF_M)
-        z_parts = [cap_score(BLOCKS - 1, 0, HALF_M)]
-        weigh(last, HALF_M, M)
-        for index, (lo, hi, tiles) in enumerate(pieces):
-            quantize_z(BLOCKS - 1, lo, hi, z_parts[index])
-            if index == 0:
-                z_parts.extend(cap_score(BLOCKS - 1, lo2, hi2) for lo2, hi2, tiles2 in pieces[1:])
+        z_first = cap_score(BLOCKS - 1, 0, HALF_M)
+        for s in range(split, SLICES):
+            look(s, HALF_M, M)
+            weigh(s, HALF_M, M)
+            if s == split:
+                quantize_z(BLOCKS - 1, 0, HALF_M, z_first)
+        z_rest = [cap_score(BLOCKS - 1, lo, hi) for lo, hi, tiles in pieces[1:]]
+        finish(*pieces[0])
+        for z, (lo, hi, tiles) in zip(z_rest, pieces[1:]):
+            quantize_z(BLOCKS - 1, lo, hi, z)
             finish(lo, hi, tiles)

@@ -65,6 +65,10 @@ def tile_list_elastography_evidence_kernel(
         w3_raw, cap, h_rows, g_rows, gate = {}, {}, {}, {}, {}
 
         nc.vector.memset(table_scales[:].bitcast(I32), 0)
+        warm_in = keep.tile([P, 1], F32, name="warm_in")
+        warm_out = keep.tile([P, 1], F32, name="warm_out")
+        nc.gpsimd.memset(warm_in[:], 0.0)
+        nc.scalar.activation(out=warm_out[:], in_=warm_in[:], func=ACT.Sigmoid)
         nc.gpsimd.memset(w2_raw_scales[:].bitcast(I32), 0)
         for q in range(4):
             nc.sync.dma_start(table_rows[32 * q : 32 * q + 4, :].bitcast(I32), tab_scales[0, 4 * q : 4 * q + 4, :].bitcast(I32))

from contextlib import ExitStack

import concourse.mybir as mybir

K, H, N, T, S, M = 512, 1536, 768, 4096, 1024, 512
FLOPS = 2 * (2 * K * H * S + H * N * M)

F32 = mybir.dt.float32
BF16 = mybir.dt.bfloat16
I32 = mybir.dt.int32
U32 = mybir.dt.uint32
U16 = mybir.dt.uint16
U8 = mybir.dt.uint8
FP8X4 = mybir.dt.float8_e4m3fn_x4
FP4X4 = mybir.dt.float4_e2m1fn_x4
ACT = mybir.ActivationFunctionType
ALU = mybir.AluOpType

P = 128
PACK = 4
PASS = P * PACK
BLOCKS = H // PASS
SLICES = BLOCKS * PACK
BANK = 512
HALF_M = M // 2
HALF_N = N // 2
G_LEAD = 4
VECTOR_BANKS = 0
PICK_LEAD = 3
SCALAR_ROUNDS = ((2, 0),)


def tile_list_elastography_evidence_kernel(
    tc, tab_words, tab_scales, offs, pos1, pos2, w1, w2_words, w2_scales, cal, thr, qual, w3, out
):
    nc = tc.nc
    with ExitStack() as ctx:
        keep = ctx.enter_context(tc.tile_pool(name="keep", bufs=1))
        work = ctx.enter_context(tc.tile_pool(name="work", bufs=2))
        psum = ctx.enter_context(tc.psum_pool(name="psum", bufs=8))

        offs_sb = keep.tile([P, S // 16], U16, name="offs_sb")
        pos1_sb = keep.tile([P, M // 16], U16, name="pos1_sb")
        pos2_sb = keep.tile([P, M // 16], U16, name="pos2_sb")
        table_words = keep.tile([P, T], U32, name="table_words")
        table_scales = keep.tile([P, T], U8, name="table_scales")
        table_rows = keep.tile([P, T], U8, name="table_rows")
        w2_rows = keep.tile([P, H], U8, name="w2_rows")
        w2_raw_words = keep.tile([P, H], U16, name="w2_raw_words")
        w2_raw_scales = keep.tile([P, H], U8, name="w2_raw_scales")
        w2_codes = keep.tile([P, H], U16, name="w2_codes", align_bytes=64)
        w2_plane = keep.tile([P, H], U8, name="w2_plane", align_bytes=64)
        cal_sb = keep.tile([P, SLICES], F32, name="cal_sb")
        thr_sb = keep.tile([P, SLICES], F32, name="thr_sb")
        v_codes = [keep.tile([P, BANK], U32, name="v_codes%d" % u, align_bytes=64) for u in range(2)]
        v_plane = [keep.tile([P, BANK], U8, name="v_plane%d" % u, align_bytes=64) for u in range(2)]
        w1_raw = [keep.tile([P, PACK, PASS], F32, name="w1_raw%d" % b) for b in range(BLOCKS)]
        w1_codes = [keep.tile([P, PASS], U32, name="w1_codes%d" % b, align_bytes=64) for b in range(BLOCKS)]
        w1_plane = [keep.tile([P, PASS], U8, name="w1_plane%d" % b, align_bytes=64) for b in range(BLOCKS)]
        w3_codes = [keep.tile([P, N], U32, name="w3_codes%d" % b, align_bytes=64) for b in range(BLOCKS)]
        w3_plane = [keep.tile([P, N], U8, name="w3_plane%d" % b, align_bytes=64) for b in range(BLOCKS)]
        z_codes = [keep.tile([P, M], U32, name="z_codes%d" % b, align_bytes=64) for b in range(BLOCKS)]
        z_plane = [keep.tile([P, M], U8, name="z_plane%d" % b, align_bytes=64) for b in range(BLOCKS)]
        score = [keep.tile([P, PACK, M], F32, name="score%d" % b) for b in range(BLOCKS)]
        w3_raw, cap, h_rows, g_rows, gate = {}, {}, {}, {}, {}

        nc.vector.memset(table_scales[:].bitcast(I32), 0)
        warm_in = keep.tile([P, 1], F32, name="warm_in")
        warm_out = keep.tile([P, 1], F32, name="warm_out")
        nc.gpsimd.memset(warm_in[:], 0.0)
        nc.scalar.activation(out=warm_out[:], in_=warm_in[:], func=ACT.Sigmoid)
        nc.gpsimd.memset(w2_raw_scales[:].bitcast(I32), 0)
        for q in range(4):
            nc.sync.dma_start(table_rows[32 * q : 32 * q + 4, :].bitcast(I32), tab_scales[0, 4 * q : 4 * q + 4, :].bitcast(I32))
        nc.sync.dma_start(offs_sb[:], offs)
        nc.sync.dma_start(w2_raw_words[:].bitcast(I32), w2_words[0].bitcast(I32))
        nc.sync.dma_start(table_words[:].bitcast(I32), tab_words[0].rearrange("p n t -> p (n t)").bitcast(I32))
        for q in range(4):
            nc.sync.dma_start(w2_rows[32 * q : 32 * q + 4, :].bitcast(I32), w2_scales[0, 4 * q : 4 * q + 4, :].bitcast(I32))

        def load_w1(b):
            nc.sync.dma_start(w1_raw[b][:], w1[:, b * PASS : (b + 1) * PASS].rearrange("(p j) c -> p j c", j=PACK))

        def load_qual(b):
            nc.sync.dma_start(score[b][:], qual[b * PASS : (b + 1) * PASS, :].rearrange("(p t) m -> p t m", t=PACK))

        def load_w3(b):
            w3_raw[b] = work.tile([P, PACK, N], F32, name="w3_raw")
            nc.sync.dma_start(w3_raw[b][:], w3[b * PASS : (b + 1) * PASS, :].rearrange("(p t) n -> p t n", t=PACK))

        load_w1(0)
        nc.sync.dma_start(pos2_sb[:], pos2)
        nc.sync.dma_start(pos1_sb[:], pos1)
        nc.sync.dma_start(cal_sb[:].rearrange("p (b t) -> p b t", t=PACK), cal.rearrange("(b p t) -> p b t", p=P, t=PACK))
        nc.sync.dma_start(thr_sb[:].rearrange("p (b t) -> p b t", t=PACK), thr.rearrange("(b p t) -> p b t", p=P, t=PACK))
        load_qual(0)
        load_w1(1)
        load_w3(0)
        load_qual(1)
        load_w1(2)
        load_w3(1)
        load_qual(2)

        def deal_words(raw, cols):
            nc.scalar.copy(
                out=w2_codes[:, cols].rearrange("p (b t m) -> p b t m", t=PACK, m=P),
                in_=raw[:].rearrange("p (b m t) -> p b t m", t=PACK, m=P),
            )

        def deal_scales(cols):
            nc.vector.tensor_copy(
                out=w2_plane[:, cols].rearrange("p (b t m) -> p b t m", t=PACK, m=P),
                in_=w2_raw_scales[:, cols].rearrange("p (b m t) -> p b t m", t=PACK, m=P),
            )

        for q in range(4):
            rows = slice(32 * q, 32 * q + 4)
            nc.vector.tensor_copy(out=table_scales[rows, :].bitcast(I32), in_=table_rows[rows, :].bitcast(I32))
        deal_words(w2_raw_words, slice(0, H))
        for u in range(2):
            nc.vector.tensor_copy(out=v_plane[u][:], in_=table_scales[:].indirect(offs_sb[:, 32 * u : 32 * u + 32]))
        for q in range(4):
            rows = slice(32 * q, 32 * q + 4)
            nc.scalar.copy(out=w2_raw_scales[rows, :].bitcast(U32), in_=w2_rows[rows, :].bitcast(U32))
        nc.vector.tensor_copy(out=v_codes[0][:], in_=table_words[:].indirect(offs_sb[:, 0:32]))
        deal_scales(slice(0, PASS))
        nc.vector.tensor_copy(out=v_codes[1][:], in_=table_words[:].indirect(offs_sb[:, 32:64]))

        def round_w1(b):
            rounded = work.tile([P, PACK * PASS], BF16, name="rounded", align_bytes=64)
            nc.vector.tensor_copy(
                out=rounded[:].rearrange("p (t m j) -> p m j t", t=PACK, j=PACK),
                in_=w1_raw[b][:].rearrange("p j (m t) -> p m j t", t=PACK),
            )
            return rounded

        def quantize_w1(b, rounded):
            nc.vector.quantize_mx(out=w1_codes[b][:].bitcast(FP8X4), scales=w1_plane[b][:], in_=rounded[:])

        def round_w3(b, u):
            rounded = work.tile([P, PACK * HALF_N], BF16, name="rounded", align_bytes=64)
            copy = nc.scalar.copy if (b, u) in SCALAR_ROUNDS else nc.vector.tensor_copy
            copy(
                out=rounded[:].rearrange("p (c i t) -> p c t i", i=2, t=PACK),
                in_=w3_raw[b][:, :, u * HALF_N : (u + 1) * HALF_N].rearrange("p t (c i) -> p c t i", i=2),
            )
            return rounded

        def quantize_w3(b, u, rounded):
            cols = slice(u * HALF_N, (u + 1) * HALF_N)
            nc.vector.quantize_mx(out=w3_codes[b][:, cols].bitcast(FP8X4), scales=w3_plane[b][:, cols], in_=rounded[:])

        def g_half(s, u):
            if u == 0:
                g_rows[s] = work.tile([P, S], F32, name="g_rows", bufs=4)
            cols = slice(s * P, (s + 1) * P)
            acc = psum.tile([P, BANK], F32, name="bank")
            nc.tensor.matmul_mx(
                out=acc[:], lhsT=w2_codes[:, cols].bitcast(FP4X4), lhsT_scale=w2_plane[:, cols],
                rhs=v_codes[u][:].bitcast(FP8X4), rhs_scale=v_plane[u][:], start=True, stop=True,
            )
            nc.scalar.copy(out=g_rows[s][:, u * BANK : (u + 1) * BANK], in_=acc[:])

        def h_half(s, u):
            b, t = divmod(s, PACK)
            if u == 0:
                h_rows[s] = work.tile([P, S], F32, name="h_rows", bufs=5)
            cols = slice(t * P, (t + 1) * P)
            acc = psum.tile([P, BANK], F32, name="bank")
            nc.tensor.matmul_mx(
                out=acc[:], lhsT=w1_codes[b][:, cols].bitcast(FP8X4), lhsT_scale=w1_plane[b][:, cols],
                rhs=v_codes[u][:].bitcast(FP8X4), rhs_scale=v_plane[u][:], start=True, stop=True,
            )
            if u == 1 and s >= SLICES - VECTOR_BANKS:
                nc.vector.tensor_copy(out=h_rows[s][:, u * BANK : (u + 1) * BANK], in_=acc[:])
            else:
                nc.scalar.copy(out=h_rows[s][:, u * BANK : (u + 1) * BANK], in_=acc[:])

        def look(s, lo, hi):
            gate[s, lo] = work.tile([P, hi - lo], F32, name="gate", bufs=4)
            nc.scalar.activation(
                out=gate[s, lo][:], in_=h_rows[s][:].indirect(pos1_sb[:, lo // 16 : hi // 16]), func=ACT.Sigmoid,
                bias=thr_sb[:, s : s + 1], scale=cal_sb[:, s : s + 1],
            )

        def pick(s):
            b, t = divmod(s, PACK)
            if t == 0:
                cap[b] = work.tile([P, PACK, M], F32, name="cap")
            nc.vector.tensor_copy(out=cap[b][:, t, :], in_=g_rows[s][:].indirect(pos2_sb[:]))

        def weigh(s, lo, hi):
            b, t = divmod(s, PACK)
            nc.vector.tensor_tensor(out=score[b][:, t, lo:hi], in0=gate[s, lo][:], in1=score[b][:, t, lo:hi], op=ALU.mult)

        def cap_score(b, lo, hi):
            cols = slice(lo, hi)
            z = work.tile([P, PACK * (hi - lo)], BF16, name="z", align_bytes=64, bufs=3)
            nc.vector.tensor_tensor(
                out=z[:].rearrange("p (c i t) -> p c t i", i=2, t=PACK),
                in0=score[b][:, :, cols].rearrange("p t (c i) -> p c t i", i=2),
                in1=cap[b][:, :, cols].rearrange("p t (c i) -> p c t i", i=2),
                op=ALU.min,
            )
            return z

        def quantize_z(b, lo, hi, z):
            cols = slice(lo, hi)
            nc.vector.quantize_mx(out=z_codes[b][:, cols].bitcast(FP8X4), scales=z_plane[b][:, cols], in_=z[:])

        for u in range(2):
            for s in range(G_LEAD):
                g_half(s, u)
        quantize_w1(0, round_w1(0))
        deal_scales(slice(PASS, H))
        h_half(0, 0)
        h_half(0, 1)

        for s in range(PICK_LEAD):
            pick(s)

        weight_jobs = {1: (1, None), 2: (0, 0), 3: (0, 1), 4: (2, None), 5: (1, 0), 6: (1, 1), 8: (2, 0), 9: (2, 1)}
        split = SLICES - PACK
        for s in range(SLICES):
            b, t = divmod(s, PACK)
            width = M if s < split else HALF_M
            if s + 1 < SLICES:
                h_half(s + 1, 0)
                h_half(s + 1, 1)
            look(s, 0, width)
            if s + G_LEAD < SLICES:
                g_half(s + G_LEAD, 0)
                g_half(s + G_LEAD, 1)
            job = weight_jobs.get(s)
            if job is not None:
                rounded = round_w1(job[0]) if job[1] is None else round_w3(*job)
            if s + PICK_LEAD < SLICES:
                pick(s + PICK_LEAD)
            if job is not None:
                if job[1] is None:
                    quantize_w1(job[0], rounded)
                else:
                    quantize_w3(job[0], job[1], rounded)
            weigh(s, 0, width)
            if job == (0, 1):
                load_w3(2)
            if t == PACK - 1 and s < split:
                z0 = cap_score(b, 0, HALF_M)
                z1 = cap_score(b, HALF_M, M)
                quantize_z(b, 0, HALF_M, z0)
                quantize_z(b, HALF_M, M, z1)

        pieces = ((0, HALF_M, 2), (HALF_M, HALF_M + P, 3), (HALF_M + P, M, 3))
        accs = {}

        def second(lo, hi, tiles, first, b):
            width = hi - lo
            if b == 0:
                accs[lo, first] = psum.tile([P, BANK], F32, name="bank")
            for e in range(tiles):
                n_cols = slice((first + e) * P, (first + e + 1) * P)
                nc.tensor.matmul_mx(
                    out=accs[lo, first][:, e * width : (e + 1) * width],
                    lhsT=w3_codes[b][:, n_cols].bitcast(FP8X4), lhsT_scale=w3_plane[b][:, n_cols],
                    rhs=z_codes[b][:, lo:hi].bitcast(FP8X4), rhs_scale=z_plane[b][:, lo:hi],
                    start=(b == 0 and e == 0), stop=(b == BLOCKS - 1 and e == tiles - 1),
                )

        def finish(lo, hi, tiles):
            width = hi - lo
            for first in range(0, N // P, tiles):
                second(lo, hi, tiles, first, BLOCKS - 1)
                result = work.tile([P, tiles, width], F32, name="result", bufs=7)
                nc.scalar.activation(
                    out=result[:].rearrange("p e m -> p (e m)"), in_=accs[lo, first][:, : tiles * width], func=ACT.Abs
                )
                nc.sync.dma_start(
                    out[first * P : (first + tiles) * P, lo:hi].rearrange("(e p) m -> p e m", p=P), result[:]
                )

        for lo, hi, tiles in pieces:
            for first in range(0, N // P, tiles):
                for b in range(BLOCKS - 1):
                    second(lo, hi, tiles, first, b)
        z_first = cap_score(BLOCKS - 1, 0, HALF_M)
        for s in range(split, SLICES):
            look(s, HALF_M, M)
            weigh(s, HALF_M, M)
            if s == split:
                quantize_z(BLOCKS - 1, 0, HALF_M, z_first)
        z_rest = [cap_score(BLOCKS - 1, lo, hi) for lo, hi, tiles in pieces[1:]]
        finish(*pieces[0])
        for z, (lo, hi, tiles) in zip(z_rest, pieces[1:]):
            quantize_z(BLOCKS - 1, lo, hi, z)
            finish(lo, hi, tiles)
